import numpy as np
import ml_dtypes

BF16 = ml_dtypes.bfloat16


def bf(x):
    return np.asarray(x, np.float32).astype(BF16)


def f32(x):
    return np.asarray(x, np.float32)


def f64(x):
    return np.asarray(x).astype(np.float64)


def striped(idx):
    return np.tile(idx.reshape(-1, 16).T, (8, 1))


def rows(idx, k):
    return np.tile(idx, (k, 1))


def look(tab, idx):
    return np.take_along_axis(f64(tab), rows(idx, len(tab)), axis=1)


K, S, V, N = 512, 2048, 512, 512


def setup_inputs():
    return {"tab": f32(np.random.standard_normal((2, K, S))), "y": f32(np.random.standard_normal((K, V))), "offs": striped(np.random.permutation(S)[:N])}


def reference(tab, y, offs):
    idx = offs[:16].T.reshape(-1)
    x = (look(tab[0], idx) - f64(y)) * (1.0 / (1.0 + np.exp(-look(tab[1], idx))))
    return x

@@ -1,0 +1,52 @@
+import concourse.mybir as mybir
+
+F32 = mybir.dt.float32
+U16 = mybir.dt.uint16
+SUBTRACT = mybir.AluOpType.subtract
+MULT = mybir.AluOpType.mult
+SIGMOID = mybir.ActivationFunctionType.Sigmoid
+
+P = 128
+LAST_PIECES = 2
+
+
+def tile_lookup_vg_subsig_out_kernel(tc, tab, y, offs, out):
+    nc = tc.nc
+    rows, places = tab.shape[1], tab.shape[2]
+    entries = y.shape[1]
+    blocks = rows // P
+
+    tab_rows = tab.rearrange("t (p b) s -> t p b s", b=blocks)
+    y_rows = y.rearrange("(p b) n -> p (b n)", b=blocks)
+    out_rows = out.rearrange("(p b) n -> p b n", b=blocks)
+
+    with tc.tile_pool(name="held", bufs=1) as held:
+        offsets = held.tile([P, entries // 16], U16, name="offsets")
+        nc.sync.dma_start(offsets[:], offs)
+        stream = held.tile([P, blocks * entries], F32, name="stream")
+        nc.sync.dma_start(stream[:], y_rows)
+
+        gates = [held.tile([P, places], F32, name=f"gates{b}") for b in range(blocks)]
+        values = [held.tile([P, places], F32, name=f"values{b}") for b in range(blocks)]
+        for b in range(blocks):
+            nc.sync.dma_start(values[b][:], tab_rows[0, :, b, :])
+            nc.sync.dma_start(gates[b][:], tab_rows[1, :, b, :])
+
+        for b in range(blocks):
+            difference = held.tile([P, entries], F32, name=f"difference{b}")
+            nc.vector.tensor_tensor(
+                difference[:],
+                values[b][:].indirect(offsets[:]),
+                stream[:, b * entries : (b + 1) * entries],
+                SUBTRACT,
+            )
+            pieces = LAST_PIECES if b == blocks - 1 else 1
+            width = entries // pieces
+            opening = held.tile([P, entries], F32, name=f"opening{b}")
+            x = held.tile([P, entries], F32, name=f"x{b}")
+            for k in range(pieces):
+                cut = slice(k * width, (k + 1) * width)
+                listed = offsets[:, k * width // 16 : (k + 1) * width // 16]
+                nc.scalar.activation(opening[:, cut], gates[b][:].indirect(listed), SIGMOID)
+                nc.vector.tensor_tensor(x[:, cut], difference[:, cut], opening[:, cut], MULT)
+                nc.sync.dma_start(out_rows[:, b, cut], x[:, cut])

@@ -7,6 +7,9 @@ MULT = mybir.AluOpType.mult
 SIGMOID = mybir.ActivationFunctionType.Sigmoid
 
 P = 128
+PER_COLUMN = 16
+STAGED_VALUES = 3
+STAGED_GATES = 2
 LAST_PIECES = 2
 
 
@@ -15,22 +18,37 @@ def tile_lookup_vg_subsig_out_kernel(tc, tab, y, offs, out):
     rows, places = tab.shape[1], tab.shape[2]
     entries = y.shape[1]
     blocks = rows // P
+    last = blocks - 1
 
-    tab_rows = tab.rearrange("t (p b) s -> t p b s", b=blocks)
+    tab_rows = tab.rearrange("t (p b) s -> t p (b s)", b=blocks)
     y_rows = y.rearrange("(p b) n -> p (b n)", b=blocks)
     out_rows = out.rearrange("(p b) n -> p b n", b=blocks)
 
-    with tc.tile_pool(name="held", bufs=1) as held:
-        offsets = held.tile([P, entries // 16], U16, name="offsets")
-        nc.sync.dma_start(offsets[:], offs)
-        stream = held.tile([P, blocks * entries], F32, name="stream")
-        nc.sync.dma_start(stream[:], y_rows)
+    def row(b):
+        return slice(b * places, (b + 1) * places)
 
-        gates = [held.tile([P, places], F32, name=f"gates{b}") for b in range(blocks)]
+    with tc.tile_pool(name="held", bufs=1) as held:
+        offsets = held.tile([P, entries // PER_COLUMN], U16, name="offsets")
+        stream = held.tile([P, blocks * entries], F32, name="stream")
+
         values = [held.tile([P, places], F32, name=f"values{b}") for b in range(blocks)]
+        gates = [held.tile([P, places], F32, name=f"gates{b}") for b in range(blocks)]
+        staged_values = held.tile([P, STAGED_VALUES * places], F32, name="staged_values")
+        staged_gates = held.tile([P, STAGED_GATES * places], F32, name="staged_gates")
+        nc.sync.dma_start(staged_values[:], tab_rows[0, :, : STAGED_VALUES * places])
+        nc.sync.dma_start(offsets[:], offs)
+        nc.sync.dma_start(stream[:], y_rows)
+        nc.sync.dma_start(staged_gates[:], tab_rows[1, :, : STAGED_GATES * places])
         for b in range(blocks):
-            nc.sync.dma_start(values[b][:], tab_rows[0, :, b, :])
-            nc.sync.dma_start(gates[b][:], tab_rows[1, :, b, :])
+            if b >= STAGED_VALUES:
+                nc.sync.dma_start(values[b][:], tab_rows[0, :, row(b)])
+            if b >= STAGED_GATES:
+                nc.sync.dma_start(gates[b][:], tab_rows[1, :, row(b)])
+
+        for b in range(STAGED_VALUES):
+            nc.vector.tensor_copy(values[b][:], staged_values[:, row(b)])
+        for b in range(STAGED_GATES):
+            nc.vector.tensor_copy(gates[b][:], staged_gates[:, row(b)])
 
         for b in range(blocks):
             difference = held.tile([P, entries], F32, name=f"difference{b}")
@@ -40,13 +58,13 @@ def tile_lookup_vg_subsig_out_kernel(tc, tab, y, offs, out):
                 stream[:, b * entries : (b + 1) * entries],
                 SUBTRACT,
             )
-            pieces = LAST_PIECES if b == blocks - 1 else 1
+            pieces = LAST_PIECES if b == last else 1
             width = entries // pieces
             opening = held.tile([P, entries], F32, name=f"opening{b}")
             x = held.tile([P, entries], F32, name=f"x{b}")
             for k in range(pieces):
                 cut = slice(k * width, (k + 1) * width)
-                listed = offsets[:, k * width // 16 : (k + 1) * width // 16]
+                listed = offsets[:, cut.start // PER_COLUMN : cut.stop // PER_COLUMN]
                 nc.scalar.activation(opening[:, cut], gates[b][:].indirect(listed), SIGMOID)
                 nc.vector.tensor_tensor(x[:, cut], difference[:, cut], opening[:, cut], MULT)
                 nc.sync.dma_start(out_rows[:, b, cut], x[:, cut])

@@ -10,7 +10,7 @@ P = 128
 PER_COLUMN = 16
 STAGED_VALUES = 3
 STAGED_GATES = 2
-LAST_PIECES = 2
+LAST_CUTS = (0, 224, 384, 512)
 
 
 def tile_lookup_vg_subsig_out_kernel(tc, tab, y, offs, out):
@@ -58,12 +58,11 @@ def tile_lookup_vg_subsig_out_kernel(tc, tab, y, offs, out):
                 stream[:, b * entries : (b + 1) * entries],
                 SUBTRACT,
             )
-            pieces = LAST_PIECES if b == last else 1
-            width = entries // pieces
+            edges = LAST_CUTS if b == last else (0, entries)
+            cuts = [slice(a, z) for a, z in zip(edges, edges[1:])]
             opening = held.tile([P, entries], F32, name=f"opening{b}")
             x = held.tile([P, entries], F32, name=f"x{b}")
-            for k in range(pieces):
-                cut = slice(k * width, (k + 1) * width)
+            for cut in cuts:
                 listed = offsets[:, cut.start // PER_COLUMN : cut.stop // PER_COLUMN]
                 nc.scalar.activation(opening[:, cut], gates[b][:].indirect(listed), SIGMOID)
                 nc.vector.tensor_tensor(x[:, cut], difference[:, cut], opening[:, cut], MULT)

@@ -8,8 +8,7 @@ SIGMOID = mybir.ActivationFunctionType.Sigmoid
 
 P = 128
 PER_COLUMN = 16
-STAGED_VALUES = 3
-STAGED_GATES = 2
+STAGED = 2
 LAST_CUTS = (0, 224, 384, 512)
 
 
@@ -20,7 +19,7 @@ def tile_lookup_vg_subsig_out_kernel(tc, tab, y, offs, out):
     blocks = rows // P
     last = blocks - 1
 
-    tab_rows = tab.rearrange("t (p b) s -> t p (b s)", b=blocks)
+    tab_rows = tab.rearrange("t (p b) s -> p t (b s)", b=blocks)
     y_rows = y.rearrange("(p b) n -> p (b n)", b=blocks)
     out_rows = out.rearrange("(p b) n -> p b n", b=blocks)
 
@@ -33,22 +32,17 @@ def tile_lookup_vg_subsig_out_kernel(tc, tab, y, offs, out):
 
         values = [held.tile([P, places], F32, name=f"values{b}") for b in range(blocks)]
         gates = [held.tile([P, places], F32, name=f"gates{b}") for b in range(blocks)]
-        staged_values = held.tile([P, STAGED_VALUES * places], F32, name="staged_values")
-        staged_gates = held.tile([P, STAGED_GATES * places], F32, name="staged_gates")
-        nc.sync.dma_start(staged_values[:], tab_rows[0, :, : STAGED_VALUES * places])
+        staged = held.tile([P, 2, STAGED * places], F32, name="staged")
+        nc.sync.dma_start(staged[:], tab_rows[:, :, : STAGED * places])
         nc.sync.dma_start(offsets[:], offs)
         nc.sync.dma_start(stream[:], y_rows)
-        nc.sync.dma_start(staged_gates[:], tab_rows[1, :, : STAGED_GATES * places])
-        for b in range(blocks):
-            if b >= STAGED_VALUES:
-                nc.sync.dma_start(values[b][:], tab_rows[0, :, row(b)])
-            if b >= STAGED_GATES:
-                nc.sync.dma_start(gates[b][:], tab_rows[1, :, row(b)])
+        for b in range(STAGED, blocks):
+            nc.sync.dma_start(values[b][:], tab_rows[:, 0, row(b)])
+            nc.sync.dma_start(gates[b][:], tab_rows[:, 1, row(b)])
 
-        for b in range(STAGED_VALUES):
-            nc.vector.tensor_copy(values[b][:], staged_values[:, row(b)])
-        for b in range(STAGED_GATES):
-            nc.vector.tensor_copy(gates[b][:], staged_gates[:, row(b)])
+        for b in range(STAGED):
+            nc.vector.tensor_copy(gates[b][:], staged[:, 1, row(b)])
+            nc.vector.tensor_copy(values[b][:], staged[:, 0, row(b)])
 
         for b in range(blocks):
             difference = held.tile([P, entries], F32, name=f"difference{b}")

@@ -8,7 +8,6 @@ SIGMOID = mybir.ActivationFunctionType.Sigmoid
 
 P = 128
 PER_COLUMN = 16
-STAGED = 2
 LAST_CUTS = (0, 224, 384, 512)
 
 
@@ -32,17 +31,11 @@ def tile_lookup_vg_subsig_out_kernel(tc, tab, y, offs, out):
 
         values = [held.tile([P, places], F32, name=f"values{b}") for b in range(blocks)]
         gates = [held.tile([P, places], F32, name=f"gates{b}") for b in range(blocks)]
-        staged = held.tile([P, 2, STAGED * places], F32, name="staged")
-        nc.sync.dma_start(staged[:], tab_rows[:, :, : STAGED * places])
-        nc.sync.dma_start(offsets[:], offs)
         nc.sync.dma_start(stream[:], y_rows)
-        for b in range(STAGED, blocks):
+        nc.sync.dma_start(offsets[:], offs)
+        for b in range(blocks):
             nc.sync.dma_start(values[b][:], tab_rows[:, 0, row(b)])
             nc.sync.dma_start(gates[b][:], tab_rows[:, 1, row(b)])
-
-        for b in range(STAGED):
-            nc.vector.tensor_copy(gates[b][:], staged[:, 1, row(b)])
-            nc.vector.tensor_copy(values[b][:], staged[:, 0, row(b)])
 
         for b in range(blocks):
             difference = held.tile([P, entries], F32, name=f"difference{b}")

@@ -8,6 +8,7 @@ SIGMOID = mybir.ActivationFunctionType.Sigmoid
 
 P = 128
 PER_COLUMN = 16
+STAGED = 3
 LAST_CUTS = (0, 224, 384, 512)
 
 
@@ -31,11 +32,16 @@ def tile_lookup_vg_subsig_out_kernel(tc, tab, y, offs, out):
 
         values = [held.tile([P, places], F32, name=f"values{b}") for b in range(blocks)]
         gates = [held.tile([P, places], F32, name=f"gates{b}") for b in range(blocks)]
-        nc.sync.dma_start(stream[:], y_rows)
+        staged = held.tile([P, STAGED * places], F32, name="staged")
+        nc.sync.dma_start(staged[:], tab_rows[:, 0, : STAGED * places])
         nc.sync.dma_start(offsets[:], offs)
+        nc.sync.dma_start(stream[:], y_rows)
         for b in range(blocks):
-            nc.sync.dma_start(values[b][:], tab_rows[:, 0, row(b)])
+            if b >= STAGED:
+                nc.sync.dma_start(values[b][:], tab_rows[:, 0, row(b)])
             nc.sync.dma_start(gates[b][:], tab_rows[:, 1, row(b)])
+        for b in range(STAGED):
+            nc.vector.tensor_copy(values[b][:], staged[:, row(b)])
 
         for b in range(blocks):
             difference = held.tile([P, entries], F32, name=f"difference{b}")

@@ -10,6 +10,7 @@ P = 128
 PER_COLUMN = 16
 STAGED = 3
 LAST_CUTS = (0, 224, 384, 512)
+HALF_CUTS = (0, 256, 512)
 
 
 def tile_lookup_vg_subsig_out_kernel(tc, tab, y, offs, out):
@@ -51,7 +52,7 @@ def tile_lookup_vg_subsig_out_kernel(tc, tab, y, offs, out):
                 stream[:, b * entries : (b + 1) * entries],
                 SUBTRACT,
             )
-            edges = LAST_CUTS if b == last else (0, entries)
+            edges = LAST_CUTS if b == last else HALF_CUTS if b > 0 else (0, entries)
             cuts = [slice(a, z) for a, z in zip(edges, edges[1:])]
             opening = held.tile([P, entries], F32, name=f"opening{b}")
             x = held.tile([P, entries], F32, name=f"x{b}")

@@ -8,7 +8,7 @@ SIGMOID = mybir.ActivationFunctionType.Sigmoid
 
 P = 128
 PER_COLUMN = 16
-STAGED = 3
+ON_VECTOR = 2
 LAST_CUTS = (0, 224, 384, 512)
 HALF_CUTS = (0, 256, 512)
 
@@ -33,16 +33,17 @@ def tile_lookup_vg_subsig_out_kernel(tc, tab, y, offs, out):
 
         values = [held.tile([P, places], F32, name=f"values{b}") for b in range(blocks)]
         gates = [held.tile([P, places], F32, name=f"gates{b}") for b in range(blocks)]
-        staged = held.tile([P, STAGED * places], F32, name="staged")
-        nc.sync.dma_start(staged[:], tab_rows[:, 0, : STAGED * places])
+        staged = held.tile([P, blocks * places], F32, name="staged")
+        nc.sync.dma_start(staged[:], tab_rows[:, 0, :])
         nc.sync.dma_start(offsets[:], offs)
         nc.sync.dma_start(stream[:], y_rows)
         for b in range(blocks):
-            if b >= STAGED:
-                nc.sync.dma_start(values[b][:], tab_rows[:, 0, row(b)])
             nc.sync.dma_start(gates[b][:], tab_rows[:, 1, row(b)])
-        for b in range(STAGED):
-            nc.vector.tensor_copy(values[b][:], staged[:, row(b)])
+        for b in range(blocks):
+            if b < ON_VECTOR:
+                nc.vector.tensor_copy(values[b][:], staged[:, row(b)])
+            else:
+                nc.scalar.copy(values[b][:], staged[:, row(b)])
 
         for b in range(blocks):
             difference = held.tile([P, entries], F32, name=f"difference{b}")
@@ -52,7 +53,7 @@ def tile_lookup_vg_subsig_out_kernel(tc, tab, y, offs, out):
                 stream[:, b * entries : (b + 1) * entries],
                 SUBTRACT,
             )
-            edges = LAST_CUTS if b == last else HALF_CUTS if b > 0 else (0, entries)
+            edges = LAST_CUTS if b == last else HALF_CUTS
             cuts = [slice(a, z) for a, z in zip(edges, edges[1:])]
             opening = held.tile([P, entries], F32, name=f"opening{b}")
             x = held.tile([P, entries], F32, name=f"x{b}")

@@ -9,8 +9,9 @@ SIGMOID = mybir.ActivationFunctionType.Sigmoid
 P = 128
 PER_COLUMN = 16
 ON_VECTOR = 2
-LAST_CUTS = (0, 224, 384, 512)
-HALF_CUTS = (0, 256, 512)
+LATE = 96
+LAST_PIECES = ((288, 512), (0, 160), (160, 288))
+HALVES = ((0, 256), (256, 512))
 
 
 def tile_lookup_vg_subsig_out_kernel(tc, tab, y, offs, out):
@@ -29,36 +30,47 @@ def tile_lookup_vg_subsig_out_kernel(tc, tab, y, offs, out):
 
     with tc.tile_pool(name="held", bufs=1) as held:
         offsets = held.tile([P, entries // PER_COLUMN], U16, name="offsets")
-        stream = held.tile([P, blocks * entries], F32, name="stream")
+        early = entries - LATE
+        stream = held.tile([P, blocks * entries - LATE], F32, name="stream")
+        results = [held.tile([P, entries], F32, name=f"x{b}") for b in range(blocks)]
+        border = LAST_PIECES[2][0]
+        late_stream = results[last][:, border - LATE // 2 : border + LATE // 2]
 
         values = [held.tile([P, places], F32, name=f"values{b}") for b in range(blocks)]
         gates = [held.tile([P, places], F32, name=f"gates{b}") for b in range(blocks)]
         staged = held.tile([P, blocks * places], F32, name="staged")
         nc.sync.dma_start(staged[:], tab_rows[:, 0, :])
         nc.sync.dma_start(offsets[:], offs)
-        nc.sync.dma_start(stream[:], y_rows)
+        nc.sync.dma_start(stream[:], y_rows[:, : blocks * entries - LATE])
         for b in range(blocks):
             nc.sync.dma_start(gates[b][:], tab_rows[:, 1, row(b)])
+        nc.sync.dma_start(late_stream, y_rows[:, blocks * entries - LATE :])
         for b in range(blocks):
             if b < ON_VECTOR:
                 nc.vector.tensor_copy(values[b][:], staged[:, row(b)])
             else:
                 nc.scalar.copy(values[b][:], staged[:, row(b)])
 
+        def listed(a, z):
+            return offsets[:, a // PER_COLUMN : z // PER_COLUMN]
+
         for b in range(blocks):
             difference = held.tile([P, entries], F32, name=f"difference{b}")
+            opening = held.tile([P, entries], F32, name=f"opening{b}")
+            x = results[b]
+            ready = early if b == last else entries
             nc.vector.tensor_tensor(
-                difference[:],
-                values[b][:].indirect(offsets[:]),
-                stream[:, b * entries : (b + 1) * entries],
+                difference[:, :ready],
+                values[b][:].indirect(listed(0, ready)),
+                stream[:, b * entries : b * entries + ready],
                 SUBTRACT,
             )
-            edges = LAST_CUTS if b == last else HALF_CUTS
-            cuts = [slice(a, z) for a, z in zip(edges, edges[1:])]
-            opening = held.tile([P, entries], F32, name=f"opening{b}")
-            x = held.tile([P, entries], F32, name=f"x{b}")
-            for cut in cuts:
-                listed = offsets[:, cut.start // PER_COLUMN : cut.stop // PER_COLUMN]
-                nc.scalar.activation(opening[:, cut], gates[b][:].indirect(listed), SIGMOID)
-                nc.vector.tensor_tensor(x[:, cut], difference[:, cut], opening[:, cut], MULT)
-                nc.sync.dma_start(out_rows[:, b, cut], x[:, cut])
+            if b == last:
+                nc.vector.tensor_tensor(
+                    difference[:, early:], values[b][:].indirect(listed(early, entries)), late_stream, SUBTRACT
+                )
+            pieces = LAST_PIECES if b == last else HALVES if b > 0 else ((0, entries),)
+            for a, z in pieces:
+                nc.scalar.activation(opening[:, a:z], gates[b][:].indirect(listed(a, z)), SIGMOID)
+                nc.vector.tensor_tensor(x[:, a:z], difference[:, a:z], opening[:, a:z], MULT)
+                nc.sync.dma_start(out_rows[:, b, a:z], x[:, a:z])

@@ -7,10 +7,11 @@ MULT = mybir.AluOpType.mult
 SIGMOID = mybir.ActivationFunctionType.Sigmoid
 
 P = 128
+DMA_BLOCK = 256
 PER_COLUMN = 16
 ON_VECTOR = 2
-LATE = 96
-LAST_PIECES = ((288, 512), (0, 160), (160, 288))
+LATE = 128
+LAST_PIECES = ((320, 512), (0, 192), (192, 320))
 HALVES = ((0, 256), (256, 512))
 
 
@@ -29,16 +30,16 @@ def tile_lookup_vg_subsig_out_kernel(tc, tab, y, offs, out):
         return slice(b * places, (b + 1) * places)
 
     with tc.tile_pool(name="held", bufs=1) as held:
-        offsets = held.tile([P, entries // PER_COLUMN], U16, name="offsets")
+        offsets = held.tile([P, entries // PER_COLUMN], U16, name="offsets", align_bytes=DMA_BLOCK)
         early = entries - LATE
-        stream = held.tile([P, blocks * entries - LATE], F32, name="stream")
-        results = [held.tile([P, entries], F32, name=f"x{b}") for b in range(blocks)]
+        stream = held.tile([P, blocks * entries - LATE], F32, name="stream", align_bytes=DMA_BLOCK)
+        results = [held.tile([P, entries], F32, name=f"x{b}", align_bytes=DMA_BLOCK) for b in range(blocks)]
         border = LAST_PIECES[2][0]
         late_stream = results[last][:, border - LATE // 2 : border + LATE // 2]
 
         values = [held.tile([P, places], F32, name=f"values{b}") for b in range(blocks)]
-        gates = [held.tile([P, places], F32, name=f"gates{b}") for b in range(blocks)]
-        staged = held.tile([P, blocks * places], F32, name="staged")
+        gates = [held.tile([P, places], F32, name=f"gates{b}", align_bytes=DMA_BLOCK) for b in range(blocks)]
+        staged = held.tile([P, blocks * places], F32, name="staged", align_bytes=DMA_BLOCK)
         nc.sync.dma_start(staged[:], tab_rows[:, 0, :])
         nc.sync.dma_start(offsets[:], offs)
         nc.sync.dma_start(stream[:], y_rows[:, : blocks * entries - LATE])

@@ -9,7 +9,7 @@ SIGMOID = mybir.ActivationFunctionType.Sigmoid
 P = 128
 DMA_BLOCK = 256
 PER_COLUMN = 16
-ON_VECTOR = 2
+ON_VECTOR = 5120
 LATE = 128
 LAST_PIECES = ((320, 512), (0, 192), (192, 320))
 HALVES = ((0, 256), (256, 512))
@@ -47,10 +47,11 @@ def tile_lookup_vg_subsig_out_kernel(tc, tab, y, offs, out):
             nc.sync.dma_start(gates[b][:], tab_rows[:, 1, row(b)])
         nc.sync.dma_start(late_stream, y_rows[:, blocks * entries - LATE :])
         for b in range(blocks):
-            if b < ON_VECTOR:
-                nc.vector.tensor_copy(values[b][:], staged[:, row(b)])
-            else:
-                nc.scalar.copy(values[b][:], staged[:, row(b)])
+            split = min(max(ON_VECTOR - b * places, 0), places)
+            if split > 0:
+                nc.vector.tensor_copy(values[b][:, :split], staged[:, row(b)][:, :split])
+            if split < places:
+                nc.scalar.copy(values[b][:, split:], staged[:, row(b)][:, split:])
 
         def listed(a, z):
             return offsets[:, a // PER_COLUMN : z // PER_COLUMN]

@@ -10,8 +10,8 @@ P = 128
 DMA_BLOCK = 256
 PER_COLUMN = 16
 ON_VECTOR = 5120
-LATE = 128
-LAST_PIECES = ((320, 512), (0, 192), (192, 320))
+LATE = 256
+LAST_PIECES = ((0, 192), (320, 512), (192, 320))
 HALVES = ((0, 256), (256, 512))
 
 
@@ -34,7 +34,7 @@ def tile_lookup_vg_subsig_out_kernel(tc, tab, y, offs, out):
         early = entries - LATE
         stream = held.tile([P, blocks * entries - LATE], F32, name="stream", align_bytes=DMA_BLOCK)
         results = [held.tile([P, entries], F32, name=f"x{b}", align_bytes=DMA_BLOCK) for b in range(blocks)]
-        border = LAST_PIECES[2][0]
+        border = LAST_PIECES[0][1]
         late_stream = results[last][:, border - LATE // 2 : border + LATE // 2]
 
         values = [held.tile([P, places], F32, name=f"values{b}") for b in range(blocks)]
@@ -68,9 +68,14 @@ def tile_lookup_vg_subsig_out_kernel(tc, tab, y, offs, out):
                 SUBTRACT,
             )
             if b == last:
-                nc.vector.tensor_tensor(
-                    difference[:, early:], values[b][:].indirect(listed(early, entries)), late_stream, SUBTRACT
-                )
+                for a in (0, LATE // 2):
+                    part = slice(early + a, early + a + LATE // 2)
+                    nc.vector.tensor_tensor(
+                        difference[:, part],
+                        values[b][:].indirect(listed(part.start, part.stop)),
+                        late_stream[:, a : a + LATE // 2],
+                        SUBTRACT,
+                    )
             pieces = LAST_PIECES if b == last else HALVES if b > 0 else ((0, entries),)
             for a, z in pieces:
                 nc.scalar.activation(opening[:, a:z], gates[b][:].indirect(listed(a, z)), SIGMOID)

@@ -10,7 +10,8 @@ P = 128
 DMA_BLOCK = 256
 PER_COLUMN = 16
 ON_VECTOR = 5120
-LATE = 256
+LATE = 320
+FIRST_LATE = 128
 LAST_PIECES = ((0, 192), (320, 512), (192, 320))
 HALVES = ((0, 256), (256, 512))
 
@@ -34,8 +35,10 @@ def tile_lookup_vg_subsig_out_kernel(tc, tab, y, offs, out):
         early = entries - LATE
         stream = held.tile([P, blocks * entries - LATE], F32, name="stream", align_bytes=DMA_BLOCK)
         results = [held.tile([P, entries], F32, name=f"x{b}", align_bytes=DMA_BLOCK) for b in range(blocks)]
-        border = LAST_PIECES[0][1]
-        late_stream = results[last][:, border - LATE // 2 : border + LATE // 2]
+        first_late = held.tile([P, FIRST_LATE], F32, name="first_late", align_bytes=DMA_BLOCK)
+        second = LATE - FIRST_LATE
+        under = second // 3
+        second_late = results[last][:, early - under : early - under + second]
 
         values = [held.tile([P, places], F32, name=f"values{b}") for b in range(blocks)]
         gates = [held.tile([P, places], F32, name=f"gates{b}", align_bytes=DMA_BLOCK) for b in range(blocks)]
@@ -45,7 +48,8 @@ def tile_lookup_vg_subsig_out_kernel(tc, tab, y, offs, out):
         nc.sync.dma_start(stream[:], y_rows[:, : blocks * entries - LATE])
         for b in range(blocks):
             nc.sync.dma_start(gates[b][:], tab_rows[:, 1, row(b)])
-        nc.sync.dma_start(late_stream, y_rows[:, blocks * entries - LATE :])
+        nc.sync.dma_start(first_late[:], y_rows[:, blocks * entries - FIRST_LATE :])
+        nc.sync.dma_start(second_late, y_rows[:, blocks * entries - LATE : blocks * entries - FIRST_LATE])
         for b in range(blocks):
             split = min(max(ON_VECTOR - b * places, 0), places)
             if split > 0:
@@ -68,15 +72,14 @@ def tile_lookup_vg_subsig_out_kernel(tc, tab, y, offs, out):
                 SUBTRACT,
             )
             if b == last:
-                for a in (0, LATE // 2):
-                    part = slice(early + a, early + a + LATE // 2)
-                    nc.vector.tensor_tensor(
-                        difference[:, part],
-                        values[b][:].indirect(listed(part.start, part.stop)),
-                        late_stream[:, a : a + LATE // 2],
-                        SUBTRACT,
-                    )
-            pieces = LAST_PIECES if b == last else HALVES if b > 0 else ((0, entries),)
+                late_parts = (
+                    (entries - FIRST_LATE, entries, first_late[:]),
+                    (early, early + under, second_late[:, :under]),
+                    (early + under, early + second, second_late[:, under:]),
+                )
+                for a, z, y_part in late_parts:
+                    nc.vector.tensor_tensor(difference[:, a:z], values[b][:].indirect(listed(a, z)), y_part, SUBTRACT)
+            pieces = LAST_PIECES if b == last else HALVES if b == last - 1 else ((0, entries),)
             for a, z in pieces:
                 nc.scalar.activation(opening[:, a:z], gates[b][:].indirect(listed(a, z)), SIGMOID)
                 nc.vector.tensor_tensor(x[:, a:z], difference[:, a:z], opening[:, a:z], MULT)

@@ -43,7 +43,7 @@ def tile_lookup_vg_subsig_out_kernel(tc, tab, y, offs, out):
         values = [held.tile([P, places], F32, name=f"values{b}") for b in range(blocks)]
         gates = [held.tile([P, places], F32, name=f"gates{b}", align_bytes=DMA_BLOCK) for b in range(blocks)]
         staged = held.tile([P, blocks * places], F32, name="staged", align_bytes=DMA_BLOCK)
-        nc.sync.dma_start(staged[:], tab_rows[:, 0, :])
+        nc.sync.dma_start(staged[:], tab_rows[:, 0, :], max_dma_last_dim=4 * places)
         nc.sync.dma_start(offsets[:], offs)
         nc.sync.dma_start(stream[:], y_rows[:, : blocks * entries - LATE])
         for b in range(blocks):

import concourse.mybir as mybir

F32 = mybir.dt.float32
U16 = mybir.dt.uint16
SUBTRACT = mybir.AluOpType.subtract
MULT = mybir.AluOpType.mult
SIGMOID = mybir.ActivationFunctionType.Sigmoid

P = 128
DMA_BLOCK = 256
PER_COLUMN = 16
ON_VECTOR = 5120
LATE = 320
FIRST_LATE = 128
LAST_PIECES = ((0, 192), (320, 512), (192, 320))
HALVES = ((0, 256), (256, 512))


def tile_lookup_vg_subsig_out_kernel(tc, tab, y, offs, out):
    nc = tc.nc
    rows, places = tab.shape[1], tab.shape[2]
    entries = y.shape[1]
    blocks = rows // P
    last = blocks - 1

    tab_rows = tab.rearrange("t (p b) s -> p t (b s)", b=blocks)
    y_rows = y.rearrange("(p b) n -> p (b n)", b=blocks)
    out_rows = out.rearrange("(p b) n -> p b n", b=blocks)

    def row(b):
        return slice(b * places, (b + 1) * places)

    with tc.tile_pool(name="held", bufs=1) as held:
        offsets = held.tile([P, entries // PER_COLUMN], U16, name="offsets", align_bytes=DMA_BLOCK)
        early = entries - LATE
        stream = held.tile([P, blocks * entries - LATE], F32, name="stream", align_bytes=DMA_BLOCK)
        results = [held.tile([P, entries], F32, name=f"x{b}", align_bytes=DMA_BLOCK) for b in range(blocks)]
        first_late = held.tile([P, FIRST_LATE], F32, name="first_late", align_bytes=DMA_BLOCK)
        second = LATE - FIRST_LATE
        under = second // 3
        second_late = results[last][:, early - under : early - under + second]

        values = [held.tile([P, places], F32, name=f"values{b}") for b in range(blocks)]
        gates = [held.tile([P, places], F32, name=f"gates{b}", align_bytes=DMA_BLOCK) for b in range(blocks)]
        staged = held.tile([P, blocks * places], F32, name="staged", align_bytes=DMA_BLOCK)
        nc.sync.dma_start(staged[:], tab_rows[:, 0, :], max_dma_last_dim=4 * places)
        nc.sync.dma_start(offsets[:], offs)
        nc.sync.dma_start(stream[:], y_rows[:, : blocks * entries - LATE])
        for b in range(blocks):
            nc.sync.dma_start(gates[b][:], tab_rows[:, 1, row(b)])
        nc.sync.dma_start(first_late[:], y_rows[:, blocks * entries - FIRST_LATE :])
        nc.sync.dma_start(second_late, y_rows[:, blocks * entries - LATE : blocks * entries - FIRST_LATE])
        for b in range(blocks):
            split = min(max(ON_VECTOR - b * places, 0), places)
            if split > 0:
                nc.vector.tensor_copy(values[b][:, :split], staged[:, row(b)][:, :split])
            if split < places:
                nc.scalar.copy(values[b][:, split:], staged[:, row(b)][:, split:])

        def listed(a, z):
            return offsets[:, a // PER_COLUMN : z // PER_COLUMN]

        for b in range(blocks):
            difference = held.tile([P, entries], F32, name=f"difference{b}")
            opening = held.tile([P, entries], F32, name=f"opening{b}")
            x = results[b]
            ready = early if b == last else entries
            nc.vector.tensor_tensor(
                difference[:, :ready],
                values[b][:].indirect(listed(0, ready)),
                stream[:, b * entries : b * entries + ready],
                SUBTRACT,
            )
            if b == last:
                late_parts = (
                    (entries - FIRST_LATE, entries, first_late[:]),
                    (early, early + under, second_late[:, :under]),
                    (early + under, early + second, second_late[:, under:]),
                )
                for a, z, y_part in late_parts:
                    nc.vector.tensor_tensor(difference[:, a:z], values[b][:].indirect(listed(a, z)), y_part, SUBTRACT)
            pieces = LAST_PIECES if b == last else HALVES if b == last - 1 else ((0, entries),)
            for a, z in pieces:
                nc.scalar.activation(opening[:, a:z], gates[b][:].indirect(listed(a, z)), SIGMOID)
                nc.vector.tensor_tensor(x[:, a:z], difference[:, a:z], opening[:, a:z], MULT)
                nc.sync.dma_start(out_rows[:, b, a:z], x[:, a:z])
